import numpy as np, ml_dtypes
CORES = [2,42,66,74,82,90,114]
N = 7
import mx_ref
KT = 2
BF = ml_dtypes.bfloat16
def setup_inputs(rng):
    def f(*shape):
        return mx_ref.flush((rng.standard_normal(shape, dtype=np.float32) * np.exp2(rng.integers(-2, 3, shape[:-1] + (1,)))).astype(BF))
    return {"x": f(N, 128, KT * 512)}
def setup_inputs_blocks(rng):
    d = setup_inputs(rng)
    for k in ("x",): d[k] = mx_ref.spread(d[k], rng, 4)
    return d
def setup_inputs_wide(rng):
    d = setup_inputs(rng)
    for k in ("x",): d[k] = mx_ref.flush((d[k].astype(np.float32) * np.exp2(rng.integers(-8, 9, (N, 1, 1))).astype(np.float32)).astype(BF))
    return d
def setup_inputs_zeros(rng):
    d = setup_inputs(rng); v = d["x"].reshape(N, 128, -1, 4).copy()
    v[np.broadcast_to((rng.random((N, 1, v.shape[2], 1)) < 0.33), v.shape)] = 0
    d["x"] = v.reshape(d["x"].shape)
    return d
def reference(x):
    Q = [[mx_ref.quantize(x[j][:, 512 * t:512 * t + 512]) for t in range(KT)] for j in range(N)]
    y = np.zeros((N, 128, N * 128), np.float32)
    for r in range(N):
        for j in range(N):
            for t in range(KT):
                p = mx_ref.matmul(Q[r][t], Q[j][t])
                y[r][:, 128 * j:128 * j + 128] = p if t == 0 else y[r][:, 128 * j:128 * j + 128] + p
    return {"y": y}

@@ -1,0 +1,145 @@
+from concourse.bass import DstId, RemoteDMATransfer
+from concourse.mybir import dt, ActivationFunctionType
+
+N = 7
+KT = 2
+COLS = 128
+SLOT = KT * COLS
+BANK = 512
+
+SELF_K = (1, 3, 5)
+HELP = ((True, (2, 4)), (True, (6,)))
+ORDER = (1, 3, 2, 5, 4, 6)
+
+SCRATCH = {
+    "xt": ("sbuf", [128, KT * 4 * COLS], "bfloat16"),
+    "q": ("sbuf", [128, N * SLOT], "float8_e4m3fn_x4"),
+    "s": ("sbuf", [128, N * SLOT], "uint8"),
+    "acc": ("psum", [128, N * BANK], "float32"),
+    "yt": ("sbuf", [128, N * COLS], "float32"),
+}
+SEMAPHORES = (["ld", "qz", "sent", "fs", "fc", "sta", "stb"]
+              + ["arr%d" % j for j in range(N)] + ["mm%d" % j for j in range(N)] + ["cp%d" % j for j in range(N)])
+
+
+def _count(mask):
+    return bin(mask).count("1")
+
+
+def _helpers(T, topo, c):
+    r = T.rank_of(c)
+    free = [h for h in range(topo.CHIPS * topo.CORES_PER_CHIP)
+            if topo.chip(h) == topo.chip(c) and T.rank_of(h) is None]
+    picked = []
+    for other, ks in HELP:
+        for h in free:
+            if (topo.die(h) != topo.die(c)) == other and all(topo.may_write(h, T.cores[(r + k) % N]) for k in ks):
+                picked.append((h, ks))
+                free.remove(h)
+                break
+    return picked
+
+
+def _common(topo, src, dsts):
+    m = topo.mask(src, dsts[0])
+    for d in dsts[1:]:
+        m &= topo.mask(src, d)
+    return m
+
+
+def _masks(T, topo, c):
+    r = T.rank_of(c)
+    away = [T.cores[(r + k) % N] for k in SELF_K]
+    near = [h for h, _ in _helpers(T, topo, c)]
+    off = _common(topo, c, away) if away else 0
+    on = (_common(topo, c, near) & ~off) if near else 0
+    return off, on
+
+
+def _xfer(topo, dsts, mask, sem, view):
+    ids = []
+    for d in dsts:
+        rid, pid, _ = topo.addr(d)
+        ids.append(DstId(rid=rid, pnc=pid))
+    return RemoteDMATransfer(dst_ids=ids, dma_engine_mask=mask, remote_sem=sem, srcs=[view],
+                             dsts=[view for _ in dsts], alu_op=0)
+
+
+def _views(T, r):
+    a, b = r * SLOT, (r + 1) * SLOT
+    return T.s[:, a:b], T.q[:, a:b].bitcast(dt.uint8)
+
+
+def _helper_program(g, core, T, topo, c, ks):
+    r = T.rank_of(c)
+    fed = _count(_masks(T, topo, c)[1])
+    dsts = [T.cores[(r + k) % N] for k in ks]
+    m = _common(topo, core, dsts)
+    for view, sem in zip(_views(T, r), (T.sem.fs, T.sem.fc)):
+        g.wait_ge(sem, fed)
+        g.remote_dma_fused([_xfer(topo, dsts, m, T.sem["arr%d" % r], view)], local_sem=T.sem.sent)
+    g.wait_ge(T.sem.sent, 2 * _count(m))
+
+
+def rank_program(g, core, T, topo):
+    r = T.rank_of(core)
+    if r is None:
+        for c in T.cores:
+            for h, ks in _helpers(T, topo, c):
+                if h == core:
+                    _helper_program(g, core, T, topo, c, ks)
+        return
+
+    own = slice(r * SLOT, (r + 1) * SLOT)
+
+    g.sync.dma_start(T.xt[:], T.x[:]).then_inc(T.sem.ld, 16)
+    g.vector.wait_ge(T.sem.ld, 16)
+    g.vector.quantize_mx(T.q[:, own], T.s[:, own], T.xt[:]).then_inc(T.sem.qz, 1)
+
+    off, on = _masks(T, topo, core)
+    away = [T.cores[(r + k) % N] for k in SELF_K]
+    near = [h for h, _ in _helpers(T, topo, core)]
+    g.wait_ge(T.sem.qz, 1)
+    for view, sem in zip(_views(T, r), (T.sem.fs, T.sem.fc)):
+        tr = []
+        if near:
+            tr.append(_xfer(topo, near, on, sem, view))
+        if away:
+            tr.append(_xfer(topo, away, off, T.sem["arr%d" % r], view))
+        g.remote_dma_fused(tr, local_sem=T.sem.sent)
+    g.wait_ge(T.sem.sent, 2 * (_count(on) + _count(off)))
+
+    g.tensor.wait_ge(T.sem.qz, 1)
+    stores = [0, 0]
+    for i, k in enumerate((0,) + ORDER):
+        j = (r - k) % N
+        if k:
+            cj = T.cores[j]
+            carrier = cj if k in SELF_K else [h for h, ks in _helpers(T, topo, cj) if k in ks][0]
+            if carrier == cj:
+                n = _count(_masks(T, topo, cj)[0])
+            else:
+                ks = [ks for h, ks in _helpers(T, topo, cj) if h == carrier][0]
+                n = _count(_common(topo, carrier, [T.cores[(j + kk) % N] for kk in ks]))
+            g.tensor.wait_ge(T.sem["arr%d" % j], 2 * n)
+        bank = T.acc[:, i * BANK:i * BANK + COLS]
+        for t in range(KT):
+            w = slice(r * SLOT + t * COLS, r * SLOT + (t + 1) * COLS)
+            m = slice(j * SLOT + t * COLS, j * SLOT + (t + 1) * COLS)
+            mm = g.tensor.matmul_mx(bank, T.q[:, w], T.s[:, w], T.q[:, m], T.s[:, m], t == 0, t == KT - 1)
+        mm.then_inc(T.sem["mm%d" % j], 1)
+
+        blk = slice(j * COLS, (j + 1) * COLS)
+        if i % 2 == 0:
+            g.vector.wait_ge(T.sem["mm%d" % j], 1)
+            g.vector.tensor_copy(T.yt[:, blk], bank).then_inc(T.sem["cp%d" % j], 1)
+            g.sync.wait_ge(T.sem["cp%d" % j], 1)
+            g.sync.dma_start(T.y[:, blk], T.yt[:, blk]).then_inc(T.sem.sta, 16)
+        else:
+            g.scalar.wait_ge(T.sem["mm%d" % j], 1)
+            g.scalar.activation(T.yt[:, blk], bank, ActivationFunctionType.Copy).then_inc(T.sem["cp%d" % j], 1)
+            g.scalar.wait_ge(T.sem["cp%d" % j], 1)
+            g.scalar.dma_start(T.y[:, blk], T.yt[:, blk]).then_inc(T.sem.stb, 16)
+        stores[i % 2] += 16
+    g.sync.wait_ge(T.sem.sta, stores[0])
+    g.scalar.wait_ge(T.sem.stb, stores[1])

@@ -7,9 +7,15 @@ COLS = 128
 SLOT = KT * COLS
 BANK = 512
 
-SELF_K = (1, 3, 5)
-HELP = ((True, (2, 4)), (True, (6,)))
-ORDER = (1, 3, 2, 5, 4, 6)
+PIECES = ("c0", "p", "c1")
+JOBS = {
+    "R": (("c0", (2, 3, 4)), ("p", (2, 3)), ("c1", (2, 3))),
+    "A": (("c0", (1, 5)), ("c1", (1,))),
+    "B": (("p", (1, 5, 4)), ("c1", (5, 4))),
+    "N": (("c0", (6,)), ("p", (6,)), ("c1", (6,))),
+}
+HELPERS = (("A", True), ("B", True), ("N", False))
+ORDER = (2, 3, 6, 1, 5, 4)
 
 SCRATCH = {
     "xt": ("sbuf", [128, KT * 4 * COLS], "bfloat16"),
@@ -18,7 +24,7 @@ SCRATCH = {
     "acc": ("psum", [128, N * BANK], "float32"),
     "yt": ("sbuf", [128, N * COLS], "float32"),
 }
-SEMAPHORES = (["ld", "qz", "sent", "fs", "fc", "sta", "stb"]
+SEMAPHORES = (["ld0", "ld1", "qz0", "qz1", "sent", "sta", "stb"] + ["fd_" + p for p in PIECES]
               + ["arr%d" % j for j in range(N)] + ["mm%d" % j for j in range(N)] + ["cp%d" % j for j in range(N)])
 
 
@@ -26,15 +32,21 @@ def _count(mask):
     return bin(mask).count("1")
 
 
+def _dsts(T, r, ks):
+    return [T.cores[(r + k) % N] for k in ks]
+
+
 def _helpers(T, topo, c):
     r = T.rank_of(c)
     free = [h for h in range(topo.CHIPS * topo.CORES_PER_CHIP)
             if topo.chip(h) == topo.chip(c) and T.rank_of(h) is None]
-    picked = []
-    for other, ks in HELP:
+    free.sort(key=lambda h: sum(1 for d in T.cores if topo.may_write(h, d)))
+    picked = {}
+    for role, other in HELPERS:
+        need = [d for _, ks in JOBS[role] for d in _dsts(T, r, ks)]
         for h in free:
-            if (topo.die(h) != topo.die(c)) == other and all(topo.may_write(h, T.cores[(r + k) % N]) for k in ks):
-                picked.append((h, ks))
+            if (topo.die(h) != topo.die(c)) == other and all(topo.may_write(h, d) for d in need):
+                picked[role] = h
                 free.remove(h)
                 break
     return picked
@@ -49,10 +61,8 @@ def _common(topo, src, dsts):
 
 def _masks(T, topo, c):
     r = T.rank_of(c)
-    away = [T.cores[(r + k) % N] for k in SELF_K]
-    near = [h for h, _ in _helpers(T, topo, c)]
-    off = _common(topo, c, away) if away else 0
-    on = (_common(topo, c, near) & ~off) if near else 0
+    off = _common(topo, c, [d for _, ks in JOBS["R"] for d in _dsts(T, r, ks)])
+    on = _common(topo, c, list(_helpers(T, topo, c).values())) & ~off
     return off, on
 
 
@@ -65,63 +75,79 @@ def _xfer(topo, dsts, mask, sem, view):
                              dsts=[view for _ in dsts], alu_op=0)
 
 
-def _views(T, r):
-    a, b = r * SLOT, (r + 1) * SLOT
-    return T.s[:, a:b], T.q[:, a:b].bitcast(dt.uint8)
+def _view(T, r, piece):
+    a = r * SLOT
+    if piece == "p":
+        return T.s[:, a:a + SLOT]
+    t = 0 if piece == "c0" else 1
+    return T.q[:, a + t * COLS:a + (t + 1) * COLS].bitcast(dt.uint8)
 
 
-def _helper_program(g, core, T, topo, c, ks):
+def _arrives(T, topo, j, k):
+    cj = T.cores[j]
+    cores = dict(_helpers(T, topo, cj))
+    cores["R"] = cj
+    n = 0
+    for role, jobs in JOBS.items():
+        for _, ks in jobs:
+            if k in ks:
+                n += _count(_masks(T, topo, cj)[0] if role == "R" else _common(topo, cores[role], _dsts(T, j, ks)))
+    return n
+
+
+def _helper_program(g, core, T, topo, c, role):
     r = T.rank_of(c)
     fed = _count(_masks(T, topo, c)[1])
-    dsts = [T.cores[(r + k) % N] for k in ks]
-    m = _common(topo, core, dsts)
-    for view, sem in zip(_views(T, r), (T.sem.fs, T.sem.fc)):
-        g.wait_ge(sem, fed)
-        g.remote_dma_fused([_xfer(topo, dsts, m, T.sem["arr%d" % r], view)], local_sem=T.sem.sent)
-    g.wait_ge(T.sem.sent, 2 * _count(m))
+    sent = 0
+    for piece, ks in JOBS[role]:
+        dsts = _dsts(T, r, ks)
+        m = _common(topo, core, dsts)
+        g.wait_ge(T.sem["fd_" + piece], fed)
+        g.remote_dma_fused([_xfer(topo, dsts, m, T.sem["arr%d" % r], _view(T, r, piece))], local_sem=T.sem.sent)
+        sent += _count(m)
+    g.wait_ge(T.sem.sent, sent)
 
 
 def rank_program(g, core, T, topo):
     r = T.rank_of(core)
     if r is None:
         for c in T.cores:
-            for h, ks in _helpers(T, topo, c):
+            for role, h in _helpers(T, topo, c).items():
                 if h == core:
-                    _helper_program(g, core, T, topo, c, ks)
+                    _helper_program(g, core, T, topo, c, role)
         return
 
-    own = slice(r * SLOT, (r + 1) * SLOT)
-
-    g.sync.dma_start(T.xt[:], T.x[:]).then_inc(T.sem.ld, 16)
-    g.vector.wait_ge(T.sem.ld, 16)
-    g.vector.quantize_mx(T.q[:, own], T.s[:, own], T.xt[:]).then_inc(T.sem.qz, 1)
+    for t, queue in enumerate((g.sync, g.scalar)):
+        queue.dma_start(T.xt[:, t * 4 * COLS:(t + 1) * 4 * COLS],
+                        T.x[:, t * 4 * COLS:(t + 1) * 4 * COLS]).then_inc(T.sem["ld%d" % t], 16)
+    for t in range(KT):
+        w = slice(r * SLOT + t * COLS, r * SLOT + (t + 1) * COLS)
+        g.vector.wait_ge(T.sem["ld%d" % t], 16)
+        g.vector.quantize_mx(T.q[:, w], T.s[:, w],
+                             T.xt[:, t * 4 * COLS:(t + 1) * 4 * COLS]).then_inc(T.sem["qz%d" % t], 1)
 
     off, on = _masks(T, topo, core)
-    away = [T.cores[(r + k) % N] for k in SELF_K]
-    near = [h for h, _ in _helpers(T, topo, core)]
-    g.wait_ge(T.sem.qz, 1)
-    for view, sem in zip(_views(T, r), (T.sem.fs, T.sem.fc)):
-        tr = []
-        if near:
-            tr.append(_xfer(topo, near, on, sem, view))
-        if away:
-            tr.append(_xfer(topo, away, off, T.sem["arr%d" % r], view))
-        g.remote_dma_fused(tr, local_sem=T.sem.sent)
-    g.wait_ge(T.sem.sent, 2 * (_count(on) + _count(off)))
+    helpers = _helpers(T, topo, core)
+    sent = 0
+    g.wait_ge(T.sem.qz0, 1)
+    for piece in PIECES:
+        if piece != "c0":
+            g.wait_ge(T.sem.qz1, 1)
+        view = _view(T, r, piece)
+        near = [helpers[role] for role, _ in HELPERS if any(p == piece for p, _ in JOBS[role])]
+        away = [d for p, ks in JOBS["R"] if p == piece for d in _dsts(T, r, ks)]
+        g.remote_dma_fused([_xfer(topo, near, on, T.sem["fd_" + piece], view),
+                            _xfer(topo, away, off, T.sem["arr%d" % r], view)], local_sem=T.sem.sent)
+        sent += _count(on) + _count(off)
+    g.wait_ge(T.sem.sent, sent)
 
-    g.tensor.wait_ge(T.sem.qz, 1)
+    g.tensor.wait_ge(T.sem.qz0, 1)
+    g.tensor.wait_ge(T.sem.qz1, 1)
     stores = [0, 0]
     for i, k in enumerate((0,) + ORDER):
         j = (r - k) % N
         if k:
-            cj = T.cores[j]
-            carrier = cj if k in SELF_K else [h for h, ks in _helpers(T, topo, cj) if k in ks][0]
-            if carrier == cj:
-                n = _count(_masks(T, topo, cj)[0])
-            else:
-                ks = [ks for h, ks in _helpers(T, topo, cj) if h == carrier][0]
-                n = _count(_common(topo, carrier, [T.cores[(j + kk) % N] for kk in ks]))
-            g.tensor.wait_ge(T.sem["arr%d" % j], 2 * n)
+            g.tensor.wait_ge(T.sem["arr%d" % j], _arrives(T, topo, j, k))
         bank = T.acc[:, i * BANK:i * BANK + COLS]
         for t in range(KT):
             w = slice(r * SLOT + t * COLS, r * SLOT + (t + 1) * COLS)

from concourse.bass import DstId, RemoteDMATransfer
from concourse.mybir import dt, ActivationFunctionType

N = 7
KT = 2
COLS = 128
SLOT = KT * COLS
BANK = 512

PIECES = ("c0", "p", "c1")
JOBS = {
    "R": (("c0", (2, 3, 4)), ("p", (2, 3)), ("c1", (2, 3))),
    "A": (("c0", (1, 5)), ("c1", (1,))),
    "B": (("p", (1, 5, 4)), ("c1", (5, 4))),
    "N": (("c0", (6,)), ("p", (6,)), ("c1", (6,))),
}
HELPERS = (("A", True), ("B", True), ("N", False))
ORDER = (2, 3, 6, 1, 5, 4)

SCRATCH = {
    "xt": ("sbuf", [128, KT * 4 * COLS], "bfloat16"),
    "q": ("sbuf", [128, N * SLOT], "float8_e4m3fn_x4"),
    "s": ("sbuf", [128, N * SLOT], "uint8"),
    "acc": ("psum", [128, N * BANK], "float32"),
    "yt": ("sbuf", [128, N * COLS], "float32"),
}
SEMAPHORES = (["ld0", "ld1", "qz0", "qz1", "sent", "sta", "stb"] + ["fd_" + p for p in PIECES]
              + ["arr%d" % j for j in range(N)] + ["mm%d" % j for j in range(N)] + ["cp%d" % j for j in range(N)])


def _count(mask):
    return bin(mask).count("1")


def _dsts(T, r, ks):
    return [T.cores[(r + k) % N] for k in ks]


def _helpers(T, topo, c):
    r = T.rank_of(c)
    free = [h for h in range(topo.CHIPS * topo.CORES_PER_CHIP)
            if topo.chip(h) == topo.chip(c) and T.rank_of(h) is None]
    free.sort(key=lambda h: sum(1 for d in T.cores if topo.may_write(h, d)))
    picked = {}
    for role, other in HELPERS:
        need = [d for _, ks in JOBS[role] for d in _dsts(T, r, ks)]
        for h in free:
            if (topo.die(h) != topo.die(c)) == other and all(topo.may_write(h, d) for d in need):
                picked[role] = h
                free.remove(h)
                break
    return picked


def _common(topo, src, dsts):
    m = topo.mask(src, dsts[0])
    for d in dsts[1:]:
        m &= topo.mask(src, d)
    return m


def _masks(T, topo, c):
    r = T.rank_of(c)
    off = _common(topo, c, [d for _, ks in JOBS["R"] for d in _dsts(T, r, ks)])
    on = _common(topo, c, list(_helpers(T, topo, c).values())) & ~off
    return off, on


def _xfer(topo, dsts, mask, sem, view):
    ids = []
    for d in dsts:
        rid, pid, _ = topo.addr(d)
        ids.append(DstId(rid=rid, pnc=pid))
    return RemoteDMATransfer(dst_ids=ids, dma_engine_mask=mask, remote_sem=sem, srcs=[view],
                             dsts=[view for _ in dsts], alu_op=0)


def _view(T, r, piece):
    a = r * SLOT
    if piece == "p":
        return T.s[:, a:a + SLOT]
    t = 0 if piece == "c0" else 1
    return T.q[:, a + t * COLS:a + (t + 1) * COLS].bitcast(dt.uint8)


def _arrives(T, topo, j, k):
    cj = T.cores[j]
    cores = dict(_helpers(T, topo, cj))
    cores["R"] = cj
    n = 0
    for role, jobs in JOBS.items():
        for _, ks in jobs:
            if k in ks:
                n += _count(_masks(T, topo, cj)[0] if role == "R" else _common(topo, cores[role], _dsts(T, j, ks)))
    return n


def _helper_program(g, core, T, topo, c, role):
    r = T.rank_of(c)
    fed = _count(_masks(T, topo, c)[1])
    sent = 0
    for piece, ks in JOBS[role]:
        dsts = _dsts(T, r, ks)
        m = _common(topo, core, dsts)
        g.wait_ge(T.sem["fd_" + piece], fed)
        g.remote_dma_fused([_xfer(topo, dsts, m, T.sem["arr%d" % r], _view(T, r, piece))], local_sem=T.sem.sent)
        sent += _count(m)
    g.wait_ge(T.sem.sent, sent)


def rank_program(g, core, T, topo):
    r = T.rank_of(core)
    if r is None:
        for c in T.cores:
            for role, h in _helpers(T, topo, c).items():
                if h == core:
                    _helper_program(g, core, T, topo, c, role)
        return

    for t, queue in enumerate((g.sync, g.scalar)):
        queue.dma_start(T.xt[:, t * 4 * COLS:(t + 1) * 4 * COLS],
                        T.x[:, t * 4 * COLS:(t + 1) * 4 * COLS]).then_inc(T.sem["ld%d" % t], 16)
    for t in range(KT):
        w = slice(r * SLOT + t * COLS, r * SLOT + (t + 1) * COLS)
        g.vector.wait_ge(T.sem["ld%d" % t], 16)
        g.vector.quantize_mx(T.q[:, w], T.s[:, w],
                             T.xt[:, t * 4 * COLS:(t + 1) * 4 * COLS]).then_inc(T.sem["qz%d" % t], 1)

    off, on = _masks(T, topo, core)
    helpers = _helpers(T, topo, core)
    sent = 0
    g.wait_ge(T.sem.qz0, 1)
    for piece in PIECES:
        if piece != "c0":
            g.wait_ge(T.sem.qz1, 1)
        view = _view(T, r, piece)
        near = [helpers[role] for role, _ in HELPERS if any(p == piece for p, _ in JOBS[role])]
        away = [d for p, ks in JOBS["R"] if p == piece for d in _dsts(T, r, ks)]
        g.remote_dma_fused([_xfer(topo, near, on, T.sem["fd_" + piece], view),
                            _xfer(topo, away, off, T.sem["arr%d" % r], view)], local_sem=T.sem.sent)
        sent += _count(on) + _count(off)
    g.wait_ge(T.sem.sent, sent)

    g.tensor.wait_ge(T.sem.qz0, 1)
    g.tensor.wait_ge(T.sem.qz1, 1)
    stores = [0, 0]
    for i, k in enumerate((0,) + ORDER):
        j = (r - k) % N
        if k:
            g.tensor.wait_ge(T.sem["arr%d" % j], _arrives(T, topo, j, k))
        bank = T.acc[:, i * BANK:i * BANK + COLS]
        for t in range(KT):
            w = slice(r * SLOT + t * COLS, r * SLOT + (t + 1) * COLS)
            m = slice(j * SLOT + t * COLS, j * SLOT + (t + 1) * COLS)
            mm = g.tensor.matmul_mx(bank, T.q[:, w], T.s[:, w], T.q[:, m], T.s[:, m], t == 0, t == KT - 1)
        mm.then_inc(T.sem["mm%d" % j], 1)

        blk = slice(j * COLS, (j + 1) * COLS)
        if i % 2 == 0:
            g.vector.wait_ge(T.sem["mm%d" % j], 1)
            g.vector.tensor_copy(T.yt[:, blk], bank).then_inc(T.sem["cp%d" % j], 1)
            g.sync.wait_ge(T.sem["cp%d" % j], 1)
            g.sync.dma_start(T.y[:, blk], T.yt[:, blk]).then_inc(T.sem.sta, 16)
        else:
            g.scalar.wait_ge(T.sem["mm%d" % j], 1)
            g.scalar.activation(T.yt[:, blk], bank, ActivationFunctionType.Copy).then_inc(T.sem["cp%d" % j], 1)
            g.scalar.wait_ge(T.sem["cp%d" % j], 1)
            g.scalar.dma_start(T.y[:, blk], T.yt[:, blk]).then_inc(T.sem.stb, 16)
        stores[i % 2] += 16
    g.sync.wait_ge(T.sem.sta, stores[0])
    g.scalar.wait_ge(T.sem.stb, stores[1])
